import numpy as np
import ml_dtypes


def mxq(x, axis, fmt="e4m3"):
    dtype, down = {"e4m3": (ml_dtypes.float8_e4m3fn, 7), "e5m2": (ml_dtypes.float8_e5m2, 14)}[fmt]
    v = np.moveaxis(np.asarray(x, np.float32).astype(ml_dtypes.bfloat16).astype(np.float64), axis, -1)
    blocks = v.reshape(v.shape[:-1] + (-1, 32))
    amax = np.abs(blocks).max(-1, keepdims=True)
    byte = np.maximum(np.where(amax > 0, np.frexp(amax)[1] - 1 + 127, 0) - down, 1)
    scale = np.exp2(byte - 127.0)
    codes = (blocks / scale).astype(np.float32).astype(dtype).astype(np.float64)
    return np.moveaxis((codes * scale).reshape(v.shape), -1, axis)


WIDE = False


def mx_kscale(k):
    if not WIDE:
        return np.ones(k)
    levels = np.array([10, -10, 5, -5, 0])
    if k % 512:
        return np.exp2(np.random.permutation(np.resize(levels, k // 32))).repeat(32)
    a = np.empty((k // 512, 16))
    for p in range(k // 512):
        a[p, :8] = np.random.permutation(np.resize(levels, 8))
        for g in range(8):
            far = levels[np.abs(levels - a[p, g]) >= 10]
            a[p, g + 8] = far[np.random.randint(len(far))]
    return np.exp2(a.ravel()).repeat(32)


def f64(x):
    return np.asarray(x).astype(np.float64)


def striped(idx):
    return np.tile(idx.reshape(-1, 16).T, (8, 1)).astype(np.uint16)


def unstriped(offs):
    return offs[:16].T.reshape(-1).astype(np.int64)


def gelu(v):
    return 0.5 * v * (1.0 + np.tanh(np.sqrt(2.0 / np.pi) * (v + 0.044715 * v**3)))


K, T, D, S, V, H, N = 1024, 2048, 8, 4096, 512, 1024, 512


def setup_inputs():
    n = np.random.standard_normal
    s = mx_kscale(K)[:, None]
    u = mx_kscale(H)
    return {
        "xT": (n((K, T)) * s).astype(np.float32),
        "w1": (n((K, H)) / np.sqrt(K) / s * u).astype(np.float32),
        "w2": (n((H, N)) / np.sqrt(H) / u[:, None]).astype(np.float32),
        "offs": striped(np.concatenate([np.random.permutation(T)[:V] for _ in range(D)])),
    }


def reference(xT, w1, w2, offs):
    idx = unstriped(offs)
    x = np.empty((K, V))
    for l in range(D):
        r = l // 4 * (4 * K // D) + l % 4 + 4 * np.arange(K // D)
        x[r] = f64(xT)[r][:, idx[l * V:(l + 1) * V]]
    xq = mxq(x, 0, "e4m3")
    h = gelu(mxq(f64(w1), 0, "e4m3").T @ xq)
    return mxq(f64(w2), 0, "e4m3").T @ mxq(h, 0, "e4m3")

@@ -1,0 +1,209 @@
+from contextlib import ExitStack
+
+import concourse.mybir as mybir
+
+K, T, LEVELS, V, H, N = 1024, 2048, 8, 512, 1024, 512
+
+F32 = mybir.dt.float32
+BF16 = mybir.dt.bfloat16
+U32 = mybir.dt.uint32
+U16 = mybir.dt.uint16
+U8 = mybir.dt.uint8
+FP8X4 = mybir.dt.float8_e4m3fn_x4
+GELU = mybir.ActivationFunctionType.Gelu_apprx_tanh
+
+P = 128
+PACK = 4
+K_PASS = P * PACK
+K_PASSES = K // K_PASS
+H_PASSES = H // K_PASS
+CHUNK = 128
+CHUNKS = V // CHUNK
+OUT_BLOCKS = N // P
+
+FLOPS = 2 * (K * H * V + H * N * V)
+
+
+def tile_picked_grid_mlp_gelu_sub_l_kernel(tc, xT, w1, w2, offs, out):
+    nc = tc.nc
+    with ExitStack() as ctx:
+        keep = ctx.enter_context(tc.tile_pool(name="keep", bufs=1))
+        psum = ctx.enter_context(tc.psum_pool(name="psum", bufs=1))
+
+        offsets = keep.tile([P, offs.shape[1]], U16, name="offsets")
+        warm_in = keep.tile([P, 1], F32, name="warm_in")
+        warm_out = keep.tile([P, 1], F32, name="warm_out")
+        tables = [keep.tile([P, T], F32, name=f"table{l}") for l in range(LEVELS)]
+        looked_up = [keep.tile([P, PACK, V], F32, name=f"looked_up{g}") for g in range(K_PASSES)]
+        x_grouped = [keep.tile([P, V, PACK], BF16, name=f"x_grouped{g}", align_bytes=64) for g in range(K_PASSES)]
+        x_codes = [keep.tile([P, V], U32, name=f"x_codes{g}", align_bytes=64) for g in range(K_PASSES)]
+        x_scales = [keep.tile([P, V], U8, name=f"x_scales{g}", align_bytes=64) for g in range(K_PASSES)]
+
+        def grid(make):
+            return [[make(b, g) for g in range(K_PASSES)] for b in range(H_PASSES)]
+
+        w1_raw = grid(lambda b, g: keep.tile([P, PACK, K_PASS], F32, name=f"w1_raw{b}{g}"))
+        w1_grouped = grid(lambda b, g: keep.tile([P, PACK, P, PACK], BF16, name=f"w1_grouped{b}{g}", align_bytes=64))
+        w1_codes = grid(lambda b, g: keep.tile([P, K_PASS], U32, name=f"w1_codes{b}{g}", align_bytes=64))
+        w1_scales = grid(lambda b, g: keep.tile([P, K_PASS], U8, name=f"w1_scales{b}{g}", align_bytes=64))
+        w2_raw = [keep.tile([P, PACK, N], F32, name=f"w2_raw{b}") for b in range(H_PASSES)]
+        w2_grouped = [keep.tile([P, N, PACK], BF16, name=f"w2_grouped{b}", align_bytes=64) for b in range(H_PASSES)]
+        w2_codes = [keep.tile([P, N], U32, name=f"w2_codes{b}", align_bytes=64) for b in range(H_PASSES)]
+        w2_scales = [keep.tile([P, N], U8, name=f"w2_scales{b}", align_bytes=64) for b in range(H_PASSES)]
+        h_grouped = [keep.tile([P, V, PACK], BF16, name=f"h_grouped{b}", align_bytes=64) for b in range(H_PASSES)]
+        h_codes = [keep.tile([P, V], U32, name=f"h_codes{b}", align_bytes=64) for b in range(H_PASSES)]
+        h_scales = [keep.tile([P, V], U8, name=f"h_scales{b}", align_bytes=64) for b in range(H_PASSES)]
+        results = [keep.tile([P, V], F32, name=f"result{m}") for m in range(OUT_BLOCKS)]
+
+        def load_w1(b, g):
+            rows = w1[g * K_PASS : (g + 1) * K_PASS, b * K_PASS : (b + 1) * K_PASS]
+            nc.sync.dma_start(out=w1_raw[b][g][:], in_=rows.rearrange("(p j) c -> p j c", j=PACK))
+
+        def load_table(l):
+            g, t = l // PACK, l % PACK
+            rows = xT[g * K_PASS : (g + 1) * K_PASS, :].rearrange("(f t) w -> f t w", t=PACK)
+            nc.sync.dma_start(out=tables[l][:], in_=rows[:, t, :])
+
+        def load_w2(b, cols):
+            rows = w2[b * K_PASS : (b + 1) * K_PASS, cols]
+            nc.sync.dma_start(out=w2_raw[b][:, :, cols], in_=rows.rearrange("(p j) n -> p j n", j=PACK))
+
+        def copy(engine, dst, src):
+            if engine == "vector":
+                nc.vector.tensor_copy(out=dst, in_=src)
+            else:
+                nc.scalar.copy(out=dst, in_=src)
+
+        def quantize(codes, scales, grouped):
+            nc.vector.quantize_mx(out=codes.bitcast(FP8X4), scales=scales, in_=grouped)
+
+        def gather(l, lo, hi):
+            g, t = l // PACK, l % PACK
+            piece = offsets[:, (l * V + lo) // 16 : (l * V + hi) // 16]
+            nc.vector.tensor_copy(out=looked_up[g][:, t, lo:hi], in_=tables[l][:].indirect(piece))
+
+        def group_x(engine, g, lo, hi):
+            copy(engine, x_grouped[g][:, lo:hi, :], looked_up[g][:, :, lo:hi].rearrange("p t v -> p v t"))
+
+        def quantize_x(g, lo, hi):
+            quantize(x_codes[g][:, lo:hi], x_scales[g][:, lo:hi], x_grouped[g][:, lo:hi, :].rearrange("p v t -> p (v t)"))
+
+        def group_w1(engine, b, g, lo, hi):
+            copy(
+                engine,
+                w1_grouped[b][g][:, :, lo:hi, :].rearrange("p t m j -> p m t j"),
+                w1_raw[b][g][:, :, PACK * lo : PACK * hi].rearrange("p j (m t) -> p m t j", t=PACK),
+            )
+
+        def quantize_w1(b, g, lo, hi):
+            cols = slice(P * lo, P * hi)
+            quantize(w1_codes[b][g][:, cols], w1_scales[b][g][:, cols], w1_grouped[b][g][:, lo:hi].rearrange("p t m j -> p (t m j)"))
+
+        def group_w2(engine, b, lo, hi):
+            copy(engine, w2_grouped[b][:, lo:hi, :], w2_raw[b][:, :, lo:hi].rearrange("p j n -> p n j"))
+
+        def quantize_w2(b, lo, hi):
+            quantize(w2_codes[b][:, lo:hi], w2_scales[b][:, lo:hi], w2_grouped[b][:, lo:hi, :].rearrange("p n j -> p (n j)"))
+
+        def first_product(pre, b, t, c):
+            w_cols = slice(t * P, (t + 1) * P)
+            x_cols = slice(c * CHUNK, (c + 1) * CHUNK)
+            for g in range(K_PASSES):
+                nc.tensor.matmul_mx(
+                    out=pre[:, t, :],
+                    lhsT=w1_codes[b][g][:, w_cols].bitcast(FP8X4),
+                    lhsT_scale=w1_scales[b][g][:, w_cols],
+                    rhs=x_codes[g][:, x_cols].bitcast(FP8X4),
+                    rhs_scale=x_scales[g][:, x_cols],
+                    start=(g == 0),
+                    stop=(g == K_PASSES - 1),
+                )
+
+        def gelu(pre, b, c):
+            nc.scalar.activation(out=h_grouped[b][:, c * CHUNK : (c + 1) * CHUNK, :], in_=pre[:].rearrange("p t n -> p n t"), func=GELU)
+
+        def quantize_h(b, lo, hi):
+            quantize(h_codes[b][:, lo:hi], h_scales[b][:, lo:hi], h_grouped[b][:, lo:hi, :].rearrange("p n t -> p (n t)"))
+
+        accs = [psum.tile([P, V], F32, name=f"acc{m}") for m in range(OUT_BLOCKS)]
+
+        def second_product(b, m):
+            cols = slice(m * P, (m + 1) * P)
+            nc.tensor.matmul_mx(
+                out=accs[m][:],
+                lhsT=w2_codes[b][:, cols].bitcast(FP8X4),
+                lhsT_scale=w2_scales[b][:, cols],
+                rhs=h_codes[b][:].bitcast(FP8X4),
+                rhs_scale=h_scales[b][:],
+                start=(b == 0),
+                stop=(b == H_PASSES - 1),
+            )
+
+        def finish(engine, m):
+            copy(engine, results[m][:], accs[m][:])
+            nc.sync.dma_start(out=out[m * P : (m + 1) * P, :], in_=results[m][:])
+
+        load_w1(0, 0)
+        nc.sync.dma_start(offsets[:], offs)
+        load_w1(0, 1)
+        for l in range(LEVELS):
+            load_table(l)
+        load_w1(1, 0)
+        load_w1(1, 1)
+        load_w2(0, slice(0, N))
+        load_w2(1, slice(0, N // 2))
+        load_w2(1, slice(N // 2, N))
+
+        nc.vector.memset(warm_in[:], 0.0)
+        nc.scalar.activation(out=warm_out[:], in_=warm_in[:], func=GELU)
+
+        group_w1("scalar", 0, 0, 0, P)
+        group_w1("vector", 0, 1, 0, P)
+        quantize_w1(0, 0, 0, PACK)
+        quantize_w1(0, 1, 0, PACK)
+        half = V // 2
+        for l in range(PACK):
+            gather(l, 0, V)
+        group_x("scalar", 0, 0, V)
+        gather(4, 0, V)
+        quantize_x(0, 0, V)
+        for l in range(5, LEVELS - 1):
+            gather(l, 0, V)
+        gather(LEVELS - 1, 0, half)
+        gather(LEVELS - 1, half, V)
+        group_x("vector", 1, 0, half)
+        group_x("scalar", 1, half, V)
+        quantize_x(1, 0, half)
+        quantize_x(1, half, V)
+
+        pres = [psum.tile([P, PACK, CHUNK], F32, name=f"pre0{c}", tag=f"pre{c}") for c in range(CHUNKS)]
+        group_w1("vector", 1, 0, 0, P // 2)
+        group_w1("scalar", 1, 0, P // 2, P)
+        for c in range(CHUNKS):
+            for t in range(PACK):
+                first_product(pres[c], 0, t, c)
+            gelu(pres[c], 0, c)
+        quantize_w1(1, 0, 0, PACK)
+        group_w1("vector", 1, 1, 0, P)
+        quantize_w1(1, 1, 0, PACK // 2)
+        quantize_w1(1, 1, PACK // 2, PACK)
+        pres = [psum.tile([P, PACK, CHUNK], F32, name=f"pre1{c}", tag=f"pre{c}") for c in range(CHUNKS)]
+        for t in range(PACK):
+            for c in range(CHUNKS):
+                first_product(pres[c], 1, t, c)
+        quantize_h(0, 0, V)
+        for c in range(CHUNKS):
+            gelu(pres[c], 1, c)
+        group_w2("vector", 0, 0, N)
+        quantize_w2(0, 0, N)
+        for m in range(OUT_BLOCKS):
+            second_product(0, m)
+        group_w2("vector", 1, 0, N // 2)
+        group_w2("scalar", 1, N // 2, N)
+        quantize_h(1, 0, V // 2)
+        quantize_w2(1, 0, N // 2)
+        quantize_h(1, V // 2, V)
+        quantize_w2(1, N // 2, N)
+        for m in range(OUT_BLOCKS):
+            second_product(1, m)
+            finish("vector" if m == 2 else "scalar", m)

@@ -14,6 +14,7 @@ GELU = mybir.ActivationFunctionType.Gelu_apprx_tanh
 
 P = 128
 PACK = 4
+LINE = 4
 K_PASS = P * PACK
 K_PASSES = K // K_PASS
 H_PASSES = H // K_PASS
@@ -53,11 +54,12 @@ def tile_picked_grid_mlp_gelu_sub_l_kernel(tc, xT, w1, w2, offs, out):
         h_grouped = [keep.tile([P, V, PACK], BF16, name=f"h_grouped{b}", align_bytes=64) for b in range(H_PASSES)]
         h_codes = [keep.tile([P, V], U32, name=f"h_codes{b}", align_bytes=64) for b in range(H_PASSES)]
         h_scales = [keep.tile([P, V], U8, name=f"h_scales{b}", align_bytes=64) for b in range(H_PASSES)]
-        results = [keep.tile([P, V], F32, name=f"result{m}") for m in range(OUT_BLOCKS)]
+        results_a = [keep.tile([P, 2, V // 2], F32, name=f"result_a{m}") for m in range(2)]
+        results_b = [keep.tile([P, V // 2], F32, name=f"result_b{m}") for m in range(OUT_BLOCKS)]
 
-        def load_w1(b, g):
-            rows = w1[g * K_PASS : (g + 1) * K_PASS, b * K_PASS : (b + 1) * K_PASS]
-            nc.sync.dma_start(out=w1_raw[b][g][:], in_=rows.rearrange("(p j) c -> p j c", j=PACK))
+        def load_w1(b, g, lo, hi):
+            rows = w1[g * K_PASS : (g + 1) * K_PASS, b * K_PASS + lo : b * K_PASS + hi]
+            nc.sync.dma_start(out=w1_raw[b][g][:, :, lo:hi], in_=rows.rearrange("(p j) c -> p j c", j=PACK))
 
         def load_table(l):
             g, t = l // PACK, l % PACK
@@ -83,7 +85,11 @@ def tile_picked_grid_mlp_gelu_sub_l_kernel(tc, xT, w1, w2, offs, out):
             nc.vector.tensor_copy(out=looked_up[g][:, t, lo:hi], in_=tables[l][:].indirect(piece))
 
         def group_x(engine, g, lo, hi):
-            copy(engine, x_grouped[g][:, lo:hi, :], looked_up[g][:, :, lo:hi].rearrange("p t v -> p v t"))
+            copy(
+                engine,
+                x_grouped[g][:, lo:hi, :].rearrange("p (c i) t -> p c t i", i=LINE),
+                looked_up[g][:, :, lo:hi].rearrange("p t (c i) -> p c t i", i=LINE),
+            )
 
         def quantize_x(g, lo, hi):
             quantize(x_codes[g][:, lo:hi], x_scales[g][:, lo:hi], x_grouped[g][:, lo:hi, :].rearrange("p v t -> p (v t)"))
@@ -91,8 +97,8 @@ def tile_picked_grid_mlp_gelu_sub_l_kernel(tc, xT, w1, w2, offs, out):
         def group_w1(engine, b, g, lo, hi):
             copy(
                 engine,
-                w1_grouped[b][g][:, :, lo:hi, :].rearrange("p t m j -> p m t j"),
-                w1_raw[b][g][:, :, PACK * lo : PACK * hi].rearrange("p j (m t) -> p m t j", t=PACK),
+                w1_grouped[b][g][:, :, lo:hi, :].rearrange("p t m j -> p m j t"),
+                w1_raw[b][g][:, :, PACK * lo : PACK * hi].rearrange("p j (m t) -> p m j t", t=PACK),
             )
 
         def quantize_w1(b, g, lo, hi):
@@ -100,7 +106,11 @@ def tile_picked_grid_mlp_gelu_sub_l_kernel(tc, xT, w1, w2, offs, out):
             quantize(w1_codes[b][g][:, cols], w1_scales[b][g][:, cols], w1_grouped[b][g][:, lo:hi].rearrange("p t m j -> p (t m j)"))
 
         def group_w2(engine, b, lo, hi):
-            copy(engine, w2_grouped[b][:, lo:hi, :], w2_raw[b][:, :, lo:hi].rearrange("p j n -> p n j"))
+            copy(
+                engine,
+                w2_grouped[b][:, lo:hi, :].rearrange("p (c i) j -> p c j i", i=LINE),
+                w2_raw[b][:, :, lo:hi].rearrange("p j (c i) -> p c j i", i=LINE),
+            )
 
         def quantize_w2(b, lo, hi):
             quantize(w2_codes[b][:, lo:hi], w2_scales[b][:, lo:hi], w2_grouped[b][:, lo:hi, :].rearrange("p n j -> p (n j)"))
@@ -125,31 +135,27 @@ def tile_picked_grid_mlp_gelu_sub_l_kernel(tc, xT, w1, w2, offs, out):
         def quantize_h(b, lo, hi):
             quantize(h_codes[b][:, lo:hi], h_scales[b][:, lo:hi], h_grouped[b][:, lo:hi, :].rearrange("p n t -> p (n t)"))
 
-        accs = [psum.tile([P, V], F32, name=f"acc{m}") for m in range(OUT_BLOCKS)]
-
-        def second_product(b, m):
+        def second_pass(acc, b, m, v_cols):
             cols = slice(m * P, (m + 1) * P)
             nc.tensor.matmul_mx(
-                out=accs[m][:],
+                out=acc,
                 lhsT=w2_codes[b][:, cols].bitcast(FP8X4),
                 lhsT_scale=w2_scales[b][:, cols],
-                rhs=h_codes[b][:].bitcast(FP8X4),
-                rhs_scale=h_scales[b][:],
+                rhs=h_codes[b][:, v_cols].bitcast(FP8X4),
+                rhs_scale=h_scales[b][:, v_cols],
                 start=(b == 0),
                 stop=(b == H_PASSES - 1),
             )
 
-        def finish(engine, m):
-            copy(engine, results[m][:], accs[m][:])
-            nc.sync.dma_start(out=out[m * P : (m + 1) * P, :], in_=results[m][:])
-
-        load_w1(0, 0)
+        half = V // 2
         nc.sync.dma_start(offsets[:], offs)
-        load_w1(0, 1)
         for l in range(LEVELS):
             load_table(l)
-        load_w1(1, 0)
-        load_w1(1, 1)
+        load_w1(0, 0, 0, K_PASS)
+        load_w1(0, 1, 0, K_PASS)
+        load_w1(1, 0, 0, K_PASS)
+        load_w1(1, 1, 0, K_PASS // 2)
+        load_w1(1, 1, K_PASS // 2, K_PASS)
         load_w2(0, slice(0, N))
         load_w2(1, slice(0, N // 2))
         load_w2(1, slice(N // 2, N))
@@ -157,53 +163,85 @@ def tile_picked_grid_mlp_gelu_sub_l_kernel(tc, xT, w1, w2, offs, out):
         nc.vector.memset(warm_in[:], 0.0)
         nc.scalar.activation(out=warm_out[:], in_=warm_in[:], func=GELU)
 
-        group_w1("scalar", 0, 0, 0, P)
-        group_w1("vector", 0, 1, 0, P)
-        quantize_w1(0, 0, 0, PACK)
-        quantize_w1(0, 1, 0, PACK)
-        half = V // 2
         for l in range(PACK):
             gather(l, 0, V)
-        group_x("scalar", 0, 0, V)
+        group_x("vector", 0, 0, half)
+        group_x("scalar", 0, half, V)
         gather(4, 0, V)
         quantize_x(0, 0, V)
-        for l in range(5, LEVELS - 1):
-            gather(l, 0, V)
-        gather(LEVELS - 1, 0, half)
-        gather(LEVELS - 1, half, V)
-        group_x("vector", 1, 0, half)
-        group_x("scalar", 1, half, V)
-        quantize_x(1, 0, half)
+        gather(5, 0, V)
+        gather(6, 0, V)
+        gather(7, half, V)
+        gather(7, 0, half)
+        group_x("vector", 1, half, V)
+        group_x("scalar", 1, 0, half // 2)
+        group_x("vector", 1, half // 2, half)
         quantize_x(1, half, V)
+        quantize_x(1, 0, half)
 
+        warm_bank = psum.tile([P, V], F32, name="warm_bank", tag="acc_b0")
+        for i in range(5):
+            nc.tensor.matmul_mx(
+                out=warm_bank[:],
+                lhsT=x_codes[1][:, 0:P].bitcast(FP8X4),
+                lhsT_scale=x_scales[1][:, 0:P],
+                rhs=x_codes[0][:].bitcast(FP8X4),
+                rhs_scale=x_scales[0][:],
+                start=True,
+                stop=True,
+            )
+
+        group_w1("scalar", 0, 0, 0, 96)
+        group_w1("vector", 0, 0, 96, P)
+        group_w1("vector", 0, 1, 0, 96)
+        group_w1("scalar", 0, 1, 96, P)
+        quantize_w1(0, 0, 0, PACK)
+        quantize_w1(0, 1, 0, PACK)
         pres = [psum.tile([P, PACK, CHUNK], F32, name=f"pre0{c}", tag=f"pre{c}") for c in range(CHUNKS)]
-        group_w1("vector", 1, 0, 0, P // 2)
-        group_w1("scalar", 1, 0, P // 2, P)
         for c in range(CHUNKS):
             for t in range(PACK):
                 first_product(pres[c], 0, t, c)
+        group_w1("scalar", 1, 0, 0, 96)
+        group_w1("vector", 1, 0, 96, P)
+        for c in range(CHUNKS):
             gelu(pres[c], 0, c)
+        group_w1("vector", 1, 1, 0, P // 2)
+        group_w1("vector", 1, 1, P // 2, P)
         quantize_w1(1, 0, 0, PACK)
-        group_w1("vector", 1, 1, 0, P)
         quantize_w1(1, 1, 0, PACK // 2)
         quantize_w1(1, 1, PACK // 2, PACK)
         pres = [psum.tile([P, PACK, CHUNK], F32, name=f"pre1{c}", tag=f"pre{c}") for c in range(CHUNKS)]
-        for t in range(PACK):
-            for c in range(CHUNKS):
-                first_product(pres[c], 1, t, c)
-        quantize_h(0, 0, V)
         for c in range(CHUNKS):
+            for t in range(PACK):
+                first_product(pres[c], 1, t, c)
             gelu(pres[c], 1, c)
-        group_w2("vector", 0, 0, N)
-        quantize_w2(0, 0, N)
-        for m in range(OUT_BLOCKS):
-            second_product(0, m)
-        group_w2("vector", 1, 0, N // 2)
-        group_w2("scalar", 1, N // 2, N)
-        quantize_h(1, 0, V // 2)
+            if c == 0:
+                group_w2("vector", 0, 0, 384)
+                group_w2("scalar", 0, 384, N)
+                quantize_h(0, 0, V)
+                quantize_w2(0, 0, N)
+                group_w2("scalar", 1, 0, 128)
+                group_w2("vector", 1, 128, 256)
+            if c == 1:
+                group_w2("vector", 1, 256, 448)
+                group_w2("scalar", 1, 448, N)
+        quantize_h(1, 0, half)
         quantize_w2(1, 0, N // 2)
-        quantize_h(1, V // 2, V)
         quantize_w2(1, N // 2, N)
+        quantize_h(1, half, V)
+
+        acc_b = [psum.tile([P, half], F32, name=f"acc_b{m}", tag=f"acc_b{m}" if m < 2 else f"pre{m - 2}") for m in range(OUT_BLOCKS)]
         for m in range(OUT_BLOCKS):
-            second_product(1, m)
-            finish("vector" if m == 2 else "scalar", m)
+            second_pass(acc_b[m][:], 0, m, slice(half, V))
+        for mp in range(2):
+            acc_a = psum.tile([P, 2, half], F32, name=f"acc_a{mp}")
+            for mi in range(2):
+                for b in range(H_PASSES):
+                    second_pass(acc_a[:, mi, :], b, 2 * mp + mi, slice(0, half))
+            copy("scalar" if mp == 0 else "vector", results_a[mp][:], acc_a[:])
+            rows = out[2 * mp * P : (2 * mp + 2) * P, 0:half]
+            nc.sync.dma_start(out=rows.rearrange("(i p) v -> p i v", i=2), in_=results_a[mp][:])
+        for m in range(OUT_BLOCKS):
+            second_pass(acc_b[m][:], 1, m, slice(half, V))
+            copy("scalar" if m % 2 == 0 else "vector", results_b[m][:], acc_b[m][:])
+            nc.sync.dma_start(out=out[m * P : (m + 1) * P, half:V], in_=results_b[m][:])

@@ -43,7 +43,9 @@ def tile_picked_grid_mlp_gelu_sub_l_kernel(tc, xT, w1, w2, offs, out):
         def grid(make):
             return [[make(b, g) for g in range(K_PASSES)] for b in range(H_PASSES)]
 
-        w1_raw = grid(lambda b, g: keep.tile([P, PACK, K_PASS], F32, name=f"w1_raw{b}{g}"))
+        w1_raw0 = keep.tile([P, PACK, H], F32, name="w1_raw0")
+        w1_raw1 = [keep.tile([P, PACK, K_PASS], F32, name=f"w1_raw1{b}") for b in range(H_PASSES)]
+        w1_raw = [[w1_raw0[:, :, b * K_PASS : (b + 1) * K_PASS], w1_raw1[b][:]] for b in range(H_PASSES)]
         w1_grouped = grid(lambda b, g: keep.tile([P, PACK, P, PACK], BF16, name=f"w1_grouped{b}{g}", align_bytes=64))
         w1_codes = grid(lambda b, g: keep.tile([P, K_PASS], U32, name=f"w1_codes{b}{g}", align_bytes=64))
         w1_scales = grid(lambda b, g: keep.tile([P, K_PASS], U8, name=f"w1_scales{b}{g}", align_bytes=64))
@@ -57,18 +59,18 @@ def tile_picked_grid_mlp_gelu_sub_l_kernel(tc, xT, w1, w2, offs, out):
         results_a = [keep.tile([P, 2, V // 2], F32, name=f"result_a{m}") for m in range(2)]
         results_b = [keep.tile([P, V // 2], F32, name=f"result_b{m}") for m in range(OUT_BLOCKS)]
 
-        def load_w1(b, g, lo, hi):
-            rows = w1[g * K_PASS : (g + 1) * K_PASS, b * K_PASS + lo : b * K_PASS + hi]
-            nc.sync.dma_start(out=w1_raw[b][g][:, :, lo:hi], in_=rows.rearrange("(p j) c -> p j c", j=PACK))
+        def load_w1(dst, g, lo, hi):
+            rows = w1[g * K_PASS : (g + 1) * K_PASS, lo:hi]
+            nc.sync.dma_start(out=dst[:], in_=rows.rearrange("(p j) c -> p j c", j=PACK))
 
         def load_table(l):
             g, t = l // PACK, l % PACK
             rows = xT[g * K_PASS : (g + 1) * K_PASS, :].rearrange("(f t) w -> f t w", t=PACK)
             nc.sync.dma_start(out=tables[l][:], in_=rows[:, t, :])
 
-        def load_w2(b, cols):
-            rows = w2[b * K_PASS : (b + 1) * K_PASS, cols]
-            nc.sync.dma_start(out=w2_raw[b][:, :, cols], in_=rows.rearrange("(p j) n -> p j n", j=PACK))
+        def load_w2(b):
+            rows = w2[b * K_PASS : (b + 1) * K_PASS, :]
+            nc.sync.dma_start(out=w2_raw[b][:], in_=rows.rearrange("(p j) n -> p j n", j=PACK))
 
         def copy(engine, dst, src):
             if engine == "vector":
@@ -148,39 +150,39 @@ def tile_picked_grid_mlp_gelu_sub_l_kernel(tc, xT, w1, w2, offs, out):
             )
 
         half = V // 2
+        load_w1(w1_raw0, 0, 0, H)
         nc.sync.dma_start(offsets[:], offs)
         for l in range(LEVELS):
             load_table(l)
-        load_w1(0, 0, 0, K_PASS)
-        load_w1(0, 1, 0, K_PASS)
-        load_w1(1, 0, 0, K_PASS)
-        load_w1(1, 1, 0, K_PASS // 2)
-        load_w1(1, 1, K_PASS // 2, K_PASS)
-        load_w2(0, slice(0, N))
-        load_w2(1, slice(0, N // 2))
-        load_w2(1, slice(N // 2, N))
+        for b in range(H_PASSES):
+            load_w1(w1_raw1[b], 1, b * K_PASS, (b + 1) * K_PASS)
+        for b in range(H_PASSES):
+            load_w2(b)
 
         nc.vector.memset(warm_in[:], 0.0)
         nc.scalar.activation(out=warm_out[:], in_=warm_in[:], func=GELU)
 
-        for l in range(PACK):
+        group_w1("scalar", 0, 0, 0, P)
+        group_w1("scalar", 1, 0, 0, P)
+        quantize_w1(0, 0, 0, PACK)
+        gather(0, 0, V)
+        quantize_w1(1, 0, 0, PACK)
+        for l in range(1, PACK):
             gather(l, 0, V)
-        group_x("vector", 0, 0, half)
-        group_x("scalar", 0, half, V)
+        group_x("scalar", 0, 0, V)
         gather(4, 0, V)
         quantize_x(0, 0, V)
         gather(5, 0, V)
         gather(6, 0, V)
-        gather(7, half, V)
         gather(7, 0, half)
-        group_x("vector", 1, half, V)
+        gather(7, half, V)
         group_x("scalar", 1, 0, half // 2)
         group_x("vector", 1, half // 2, half)
-        quantize_x(1, half, V)
+        group_x("scalar", 1, half, V)
         quantize_x(1, 0, half)
 
         warm_bank = psum.tile([P, V], F32, name="warm_bank", tag="acc_b0")
-        for i in range(5):
+        for i in range(4):
             nc.tensor.matmul_mx(
                 out=warm_bank[:],
                 lhsT=x_codes[1][:, 0:P].bitcast(FP8X4),
@@ -191,42 +193,36 @@ def tile_picked_grid_mlp_gelu_sub_l_kernel(tc, xT, w1, w2, offs, out):
                 stop=True,
             )
 
-        group_w1("scalar", 0, 0, 0, 96)
-        group_w1("vector", 0, 0, 96, P)
         group_w1("vector", 0, 1, 0, 96)
         group_w1("scalar", 0, 1, 96, P)
-        quantize_w1(0, 0, 0, PACK)
+        quantize_x(1, half, V)
         quantize_w1(0, 1, 0, PACK)
         pres = [psum.tile([P, PACK, CHUNK], F32, name=f"pre0{c}", tag=f"pre{c}") for c in range(CHUNKS)]
         for c in range(CHUNKS):
             for t in range(PACK):
                 first_product(pres[c], 0, t, c)
-        group_w1("scalar", 1, 0, 0, 96)
-        group_w1("vector", 1, 0, 96, P)
+        group_w1("vector", 1, 1, 0, 80)
+        group_w1("scalar", 1, 1, 80, P)
         for c in range(CHUNKS):
             gelu(pres[c], 0, c)
-        group_w1("vector", 1, 1, 0, P // 2)
-        group_w1("vector", 1, 1, P // 2, P)
-        quantize_w1(1, 0, 0, PACK)
         quantize_w1(1, 1, 0, PACK // 2)
         quantize_w1(1, 1, PACK // 2, PACK)
+        group_w2("vector", 0, 0, N)
+        quantize_w2(0, 0, N)
         pres = [psum.tile([P, PACK, CHUNK], F32, name=f"pre1{c}", tag=f"pre{c}") for c in range(CHUNKS)]
         for c in range(CHUNKS):
             for t in range(PACK):
                 first_product(pres[c], 1, t, c)
             gelu(pres[c], 1, c)
             if c == 0:
-                group_w2("vector", 0, 0, 384)
-                group_w2("scalar", 0, 384, N)
-                quantize_h(0, 0, V)
-                quantize_w2(0, 0, N)
-                group_w2("scalar", 1, 0, 128)
-                group_w2("vector", 1, 128, 256)
+                group_w2("scalar", 1, 0, 64)
             if c == 1:
-                group_w2("vector", 1, 256, 448)
-                group_w2("scalar", 1, 448, N)
-        quantize_h(1, 0, half)
+                group_w2("scalar", 1, 320, N)
+        group_w2("vector", 1, 64, 256)
+        quantize_h(0, 0, V)
+        group_w2("vector", 1, 256, 320)
         quantize_w2(1, 0, N // 2)
+        quantize_h(1, 0, half)
         quantize_w2(1, N // 2, N)
         quantize_h(1, half, V)
 
@@ -238,10 +234,10 @@ def tile_picked_grid_mlp_gelu_sub_l_kernel(tc, xT, w1, w2, offs, out):
             for mi in range(2):
                 for b in range(H_PASSES):
                     second_pass(acc_a[:, mi, :], b, 2 * mp + mi, slice(0, half))
-            copy("scalar" if mp == 0 else "vector", results_a[mp][:], acc_a[:])
+            copy("scalar", results_a[mp][:], acc_a[:])
             rows = out[2 * mp * P : (2 * mp + 2) * P, 0:half]
             nc.sync.dma_start(out=rows.rearrange("(i p) v -> p i v", i=2), in_=results_a[mp][:])
         for m in range(OUT_BLOCKS):
             second_pass(acc_b[m][:], 1, m, slice(half, V))
-            copy("scalar" if m % 2 == 0 else "vector", results_b[m][:], acc_b[m][:])
+            copy("vector" if m % 2 == 0 else "scalar", results_b[m][:], acc_b[m][:])
             nc.sync.dma_start(out=out[m * P : (m + 1) * P, half:V], in_=results_b[m][:])

@@ -43,9 +43,7 @@ def tile_picked_grid_mlp_gelu_sub_l_kernel(tc, xT, w1, w2, offs, out):
         def grid(make):
             return [[make(b, g) for g in range(K_PASSES)] for b in range(H_PASSES)]
 
-        w1_raw0 = keep.tile([P, PACK, H], F32, name="w1_raw0")
-        w1_raw1 = [keep.tile([P, PACK, K_PASS], F32, name=f"w1_raw1{b}") for b in range(H_PASSES)]
-        w1_raw = [[w1_raw0[:, :, b * K_PASS : (b + 1) * K_PASS], w1_raw1[b][:]] for b in range(H_PASSES)]
+        w1_raw = grid(lambda b, g: keep.tile([P, PACK, K_PASS], F32, name=f"w1_raw{b}{g}"))
         w1_grouped = grid(lambda b, g: keep.tile([P, PACK, P, PACK], BF16, name=f"w1_grouped{b}{g}", align_bytes=64))
         w1_codes = grid(lambda b, g: keep.tile([P, K_PASS], U32, name=f"w1_codes{b}{g}", align_bytes=64))
         w1_scales = grid(lambda b, g: keep.tile([P, K_PASS], U8, name=f"w1_scales{b}{g}", align_bytes=64))
@@ -56,21 +54,20 @@ def tile_picked_grid_mlp_gelu_sub_l_kernel(tc, xT, w1, w2, offs, out):
         h_grouped = [keep.tile([P, V, PACK], BF16, name=f"h_grouped{b}", align_bytes=64) for b in range(H_PASSES)]
         h_codes = [keep.tile([P, V], U32, name=f"h_codes{b}", align_bytes=64) for b in range(H_PASSES)]
         h_scales = [keep.tile([P, V], U8, name=f"h_scales{b}", align_bytes=64) for b in range(H_PASSES)]
-        results_a = [keep.tile([P, 2, V // 2], F32, name=f"result_a{m}") for m in range(2)]
-        results_b = [keep.tile([P, V // 2], F32, name=f"result_b{m}") for m in range(OUT_BLOCKS)]
+        results = [keep.tile([P, V], F32, name=f"result{m}") for m in range(OUT_BLOCKS)]
 
-        def load_w1(dst, g, lo, hi):
-            rows = w1[g * K_PASS : (g + 1) * K_PASS, lo:hi]
-            nc.sync.dma_start(out=dst[:], in_=rows.rearrange("(p j) c -> p j c", j=PACK))
+        def load_w1(b, g):
+            rows = w1[g * K_PASS : (g + 1) * K_PASS, b * K_PASS : (b + 1) * K_PASS]
+            nc.sync.dma_start(out=w1_raw[b][g][:], in_=rows.rearrange("(p j) c -> p j c", j=PACK))
 
         def load_table(l):
             g, t = l // PACK, l % PACK
             rows = xT[g * K_PASS : (g + 1) * K_PASS, :].rearrange("(f t) w -> f t w", t=PACK)
             nc.sync.dma_start(out=tables[l][:], in_=rows[:, t, :])
 
-        def load_w2(b):
-            rows = w2[b * K_PASS : (b + 1) * K_PASS, :]
-            nc.sync.dma_start(out=w2_raw[b][:], in_=rows.rearrange("(p j) n -> p j n", j=PACK))
+        def load_w2(b, lo, hi):
+            rows = w2[b * K_PASS : (b + 1) * K_PASS, lo:hi]
+            nc.sync.dma_start(out=w2_raw[b][:, :, lo:hi], in_=rows.rearrange("(p j) n -> p j n", j=PACK))
 
         def copy(engine, dst, src):
             if engine == "vector":
@@ -149,95 +146,95 @@ def tile_picked_grid_mlp_gelu_sub_l_kernel(tc, xT, w1, w2, offs, out):
                 stop=(b == H_PASSES - 1),
             )
 
+        warm_bank = psum.tile([P, V], F32, name="warm_bank", tag="acc0")
+
+        def warm_up(codes, scales, col=0):
+            for i in range(3):
+                nc.tensor.matmul_mx(
+                    out=warm_bank[:],
+                    lhsT=codes[:, col : col + P].bitcast(FP8X4),
+                    lhsT_scale=scales[:, col : col + P],
+                    rhs=x_codes[0][:].bitcast(FP8X4),
+                    rhs_scale=x_scales[0][:],
+                    start=True,
+                    stop=True,
+                )
+
         half = V // 2
-        load_w1(w1_raw0, 0, 0, H)
         nc.sync.dma_start(offsets[:], offs)
         for l in range(LEVELS):
             load_table(l)
         for b in range(H_PASSES):
-            load_w1(w1_raw1[b], 1, b * K_PASS, (b + 1) * K_PASS)
-        for b in range(H_PASSES):
-            load_w2(b)
+            for g in range(K_PASSES):
+                load_w1(b, g)
+        load_w2(0, 0, N)
+        load_w2(1, 0, half)
+        load_w2(1, half, N)
 
         nc.vector.memset(warm_in[:], 0.0)
         nc.scalar.activation(out=warm_out[:], in_=warm_in[:], func=GELU)
 
-        group_w1("scalar", 0, 0, 0, P)
-        group_w1("scalar", 1, 0, 0, P)
-        quantize_w1(0, 0, 0, PACK)
-        gather(0, 0, V)
-        quantize_w1(1, 0, 0, PACK)
-        for l in range(1, PACK):
+        for l in range(PACK):
             gather(l, 0, V)
         group_x("scalar", 0, 0, V)
         gather(4, 0, V)
-        quantize_x(0, 0, V)
         gather(5, 0, V)
+        quantize_x(0, 0, V)
         gather(6, 0, V)
-        gather(7, 0, half)
         gather(7, half, V)
-        group_x("scalar", 1, 0, half // 2)
-        group_x("vector", 1, half // 2, half)
-        group_x("scalar", 1, half, V)
+        gather(7, 0, half)
+        group_x("scalar", 1, half, 384)
+        group_x("vector", 1, 384, V)
+        group_x("scalar", 1, 0, 192)
+        group_x("vector", 1, 192, half)
+        quantize_x(1, half, V)
         quantize_x(1, 0, half)
 
-        warm_bank = psum.tile([P, V], F32, name="warm_bank", tag="acc_b0")
-        for i in range(4):
-            nc.tensor.matmul_mx(
-                out=warm_bank[:],
-                lhsT=x_codes[1][:, 0:P].bitcast(FP8X4),
-                lhsT_scale=x_scales[1][:, 0:P],
-                rhs=x_codes[0][:].bitcast(FP8X4),
-                rhs_scale=x_scales[0][:],
-                start=True,
-                stop=True,
-            )
-
-        group_w1("vector", 0, 1, 0, 96)
-        group_w1("scalar", 0, 1, 96, P)
-        quantize_x(1, half, V)
+        warm_up(x_codes[1], x_scales[1], half)
+        group_w1("scalar", 0, 0, 0, 32)
+        group_w1("vector", 0, 0, 32, P)
+        quantize_w1(0, 0, 0, PACK)
+        warm_up(w1_codes[0][0], w1_scales[0][0])
+        group_w1("scalar", 0, 1, 0, 48)
+        group_w1("vector", 0, 1, 48, P)
         quantize_w1(0, 1, 0, PACK)
         pres = [psum.tile([P, PACK, CHUNK], F32, name=f"pre0{c}", tag=f"pre{c}") for c in range(CHUNKS)]
         for c in range(CHUNKS):
             for t in range(PACK):
                 first_product(pres[c], 0, t, c)
-        group_w1("vector", 1, 1, 0, 80)
-        group_w1("scalar", 1, 1, 80, P)
-        for c in range(CHUNKS):
-            gelu(pres[c], 0, c)
+        group_w1("scalar", 1, 0, 0, 48)
+        group_w1("vector", 1, 0, 48, P)
+        quantize_w1(1, 0, 0, PACK)
+        gelu(pres[0], 0, 0)
+        gelu(pres[1], 0, 1)
+        group_w1("scalar", 1, 1, 0, 32)
+        group_w1("vector", 1, 1, 32, P)
+        gelu(pres[2], 0, 2)
+        gelu(pres[3], 0, 3)
         quantize_w1(1, 1, 0, PACK // 2)
         quantize_w1(1, 1, PACK // 2, PACK)
-        group_w2("vector", 0, 0, N)
-        quantize_w2(0, 0, N)
         pres = [psum.tile([P, PACK, CHUNK], F32, name=f"pre1{c}", tag=f"pre{c}") for c in range(CHUNKS)]
         for c in range(CHUNKS):
             for t in range(PACK):
                 first_product(pres[c], 1, t, c)
-            gelu(pres[c], 1, c)
-            if c == 0:
-                group_w2("scalar", 1, 0, 64)
-            if c == 1:
-                group_w2("scalar", 1, 320, N)
-        group_w2("vector", 1, 64, 256)
+        group_w2("vector", 0, 0, N)
         quantize_h(0, 0, V)
-        group_w2("vector", 1, 256, 320)
-        quantize_w2(1, 0, N // 2)
+        quantize_w2(0, 0, N)
+        group_w2("vector", 1, 0, half)
+        gelu(pres[0], 1, 0)
+        gelu(pres[1], 1, 1)
         quantize_h(1, 0, half)
-        quantize_w2(1, N // 2, N)
+        quantize_w2(1, 0, half)
+        gelu(pres[2], 1, 2)
+        gelu(pres[3], 1, 3)
         quantize_h(1, half, V)
-
-        acc_b = [psum.tile([P, half], F32, name=f"acc_b{m}", tag=f"acc_b{m}" if m < 2 else f"pre{m - 2}") for m in range(OUT_BLOCKS)]
+        group_w2("vector", 1, half + 192, N)
+        group_w2("scalar", 1, half, half + 192)
+        quantize_w2(1, half, N)
+        accs = [psum.tile([P, V], F32, name=f"acc{m}") for m in range(OUT_BLOCKS)]
+        for b in range(H_PASSES):
+            for m in range(OUT_BLOCKS):
+                second_pass(accs[m][:], b, m, slice(0, V))
         for m in range(OUT_BLOCKS):
-            second_pass(acc_b[m][:], 0, m, slice(half, V))
-        for mp in range(2):
-            acc_a = psum.tile([P, 2, half], F32, name=f"acc_a{mp}")
-            for mi in range(2):
-                for b in range(H_PASSES):
-                    second_pass(acc_a[:, mi, :], b, 2 * mp + mi, slice(0, half))
-            copy("scalar", results_a[mp][:], acc_a[:])
-            rows = out[2 * mp * P : (2 * mp + 2) * P, 0:half]
-            nc.sync.dma_start(out=rows.rearrange("(i p) v -> p i v", i=2), in_=results_a[mp][:])
-        for m in range(OUT_BLOCKS):
-            second_pass(acc_b[m][:], 1, m, slice(half, V))
-            copy("vector" if m % 2 == 0 else "scalar", results_b[m][:], acc_b[m][:])
-            nc.sync.dma_start(out=out[m * P : (m + 1) * P, half:V], in_=results_b[m][:])
+            copy("scalar" if m % 2 == 0 else "vector", results[m][:], accs[m][:])
+            nc.sync.dma_start(out=out[m * P : (m + 1) * P, :], in_=results[m][:])

@@ -148,12 +148,12 @@ def tile_picked_grid_mlp_gelu_sub_l_kernel(tc, xT, w1, w2, offs, out):
 
         warm_bank = psum.tile([P, V], F32, name="warm_bank", tag="acc0")
 
-        def warm_up(codes, scales, col=0):
+        def warm_up(codes, scales):
             for i in range(3):
                 nc.tensor.matmul_mx(
                     out=warm_bank[:],
-                    lhsT=codes[:, col : col + P].bitcast(FP8X4),
-                    lhsT_scale=scales[:, col : col + P],
+                    lhsT=codes[:, 0:P].bitcast(FP8X4),
+                    lhsT_scale=scales[:, 0:P],
                     rhs=x_codes[0][:].bitcast(FP8X4),
                     rhs_scale=x_scales[0][:],
                     start=True,
@@ -190,7 +190,6 @@ def tile_picked_grid_mlp_gelu_sub_l_kernel(tc, xT, w1, w2, offs, out):
         quantize_x(1, half, V)
         quantize_x(1, 0, half)
 
-        warm_up(x_codes[1], x_scales[1], half)
         group_w1("scalar", 0, 0, 0, 32)
         group_w1("vector", 0, 0, 32, P)
         quantize_w1(0, 0, 0, PACK)
@@ -205,6 +204,7 @@ def tile_picked_grid_mlp_gelu_sub_l_kernel(tc, xT, w1, w2, offs, out):
         group_w1("scalar", 1, 0, 0, 48)
         group_w1("vector", 1, 0, 48, P)
         quantize_w1(1, 0, 0, PACK)
+        warm_up(w1_codes[1][0], w1_scales[1][0])
         gelu(pres[0], 0, 0)
         gelu(pres[1], 0, 1)
         group_w1("scalar", 1, 1, 0, 32)

from contextlib import ExitStack

import concourse.mybir as mybir

K, T, LEVELS, V, H, N = 1024, 2048, 8, 512, 1024, 512

F32 = mybir.dt.float32
BF16 = mybir.dt.bfloat16
U32 = mybir.dt.uint32
U16 = mybir.dt.uint16
U8 = mybir.dt.uint8
FP8X4 = mybir.dt.float8_e4m3fn_x4
GELU = mybir.ActivationFunctionType.Gelu_apprx_tanh

P = 128
PACK = 4
LINE = 4
K_PASS = P * PACK
K_PASSES = K // K_PASS
H_PASSES = H // K_PASS
CHUNK = 128
CHUNKS = V // CHUNK
OUT_BLOCKS = N // P

FLOPS = 2 * (K * H * V + H * N * V)


def tile_picked_grid_mlp_gelu_sub_l_kernel(tc, xT, w1, w2, offs, out):
    nc = tc.nc
    with ExitStack() as ctx:
        keep = ctx.enter_context(tc.tile_pool(name="keep", bufs=1))
        psum = ctx.enter_context(tc.psum_pool(name="psum", bufs=1))

        offsets = keep.tile([P, offs.shape[1]], U16, name="offsets")
        warm_in = keep.tile([P, 1], F32, name="warm_in")
        warm_out = keep.tile([P, 1], F32, name="warm_out")
        tables = [keep.tile([P, T], F32, name=f"table{l}") for l in range(LEVELS)]
        looked_up = [keep.tile([P, PACK, V], F32, name=f"looked_up{g}") for g in range(K_PASSES)]
        x_grouped = [keep.tile([P, V, PACK], BF16, name=f"x_grouped{g}", align_bytes=64) for g in range(K_PASSES)]
        x_codes = [keep.tile([P, V], U32, name=f"x_codes{g}", align_bytes=64) for g in range(K_PASSES)]
        x_scales = [keep.tile([P, V], U8, name=f"x_scales{g}", align_bytes=64) for g in range(K_PASSES)]

        def grid(make):
            return [[make(b, g) for g in range(K_PASSES)] for b in range(H_PASSES)]

        w1_raw = grid(lambda b, g: keep.tile([P, PACK, K_PASS], F32, name=f"w1_raw{b}{g}"))
        w1_grouped = grid(lambda b, g: keep.tile([P, PACK, P, PACK], BF16, name=f"w1_grouped{b}{g}", align_bytes=64))
        w1_codes = grid(lambda b, g: keep.tile([P, K_PASS], U32, name=f"w1_codes{b}{g}", align_bytes=64))
        w1_scales = grid(lambda b, g: keep.tile([P, K_PASS], U8, name=f"w1_scales{b}{g}", align_bytes=64))
        w2_raw = [keep.tile([P, PACK, N], F32, name=f"w2_raw{b}") for b in range(H_PASSES)]
        w2_grouped = [keep.tile([P, N, PACK], BF16, name=f"w2_grouped{b}", align_bytes=64) for b in range(H_PASSES)]
        w2_codes = [keep.tile([P, N], U32, name=f"w2_codes{b}", align_bytes=64) for b in range(H_PASSES)]
        w2_scales = [keep.tile([P, N], U8, name=f"w2_scales{b}", align_bytes=64) for b in range(H_PASSES)]
        h_grouped = [keep.tile([P, V, PACK], BF16, name=f"h_grouped{b}", align_bytes=64) for b in range(H_PASSES)]
        h_codes = [keep.tile([P, V], U32, name=f"h_codes{b}", align_bytes=64) for b in range(H_PASSES)]
        h_scales = [keep.tile([P, V], U8, name=f"h_scales{b}", align_bytes=64) for b in range(H_PASSES)]
        results = [keep.tile([P, V], F32, name=f"result{m}") for m in range(OUT_BLOCKS)]

        def load_w1(b, g):
            rows = w1[g * K_PASS : (g + 1) * K_PASS, b * K_PASS : (b + 1) * K_PASS]
            nc.sync.dma_start(out=w1_raw[b][g][:], in_=rows.rearrange("(p j) c -> p j c", j=PACK))

        def load_table(l):
            g, t = l // PACK, l % PACK
            rows = xT[g * K_PASS : (g + 1) * K_PASS, :].rearrange("(f t) w -> f t w", t=PACK)
            nc.sync.dma_start(out=tables[l][:], in_=rows[:, t, :])

        def load_w2(b, lo, hi):
            rows = w2[b * K_PASS : (b + 1) * K_PASS, lo:hi]
            nc.sync.dma_start(out=w2_raw[b][:, :, lo:hi], in_=rows.rearrange("(p j) n -> p j n", j=PACK))

        def copy(engine, dst, src):
            if engine == "vector":
                nc.vector.tensor_copy(out=dst, in_=src)
            else:
                nc.scalar.copy(out=dst, in_=src)

        def quantize(codes, scales, grouped):
            nc.vector.quantize_mx(out=codes.bitcast(FP8X4), scales=scales, in_=grouped)

        def gather(l, lo, hi):
            g, t = l // PACK, l % PACK
            piece = offsets[:, (l * V + lo) // 16 : (l * V + hi) // 16]
            nc.vector.tensor_copy(out=looked_up[g][:, t, lo:hi], in_=tables[l][:].indirect(piece))

        def group_x(engine, g, lo, hi):
            copy(
                engine,
                x_grouped[g][:, lo:hi, :].rearrange("p (c i) t -> p c t i", i=LINE),
                looked_up[g][:, :, lo:hi].rearrange("p t (c i) -> p c t i", i=LINE),
            )

        def quantize_x(g, lo, hi):
            quantize(x_codes[g][:, lo:hi], x_scales[g][:, lo:hi], x_grouped[g][:, lo:hi, :].rearrange("p v t -> p (v t)"))

        def group_w1(engine, b, g, lo, hi):
            copy(
                engine,
                w1_grouped[b][g][:, :, lo:hi, :].rearrange("p t m j -> p m j t"),
                w1_raw[b][g][:, :, PACK * lo : PACK * hi].rearrange("p j (m t) -> p m j t", t=PACK),
            )

        def quantize_w1(b, g, lo, hi):
            cols = slice(P * lo, P * hi)
            quantize(w1_codes[b][g][:, cols], w1_scales[b][g][:, cols], w1_grouped[b][g][:, lo:hi].rearrange("p t m j -> p (t m j)"))

        def group_w2(engine, b, lo, hi):
            copy(
                engine,
                w2_grouped[b][:, lo:hi, :].rearrange("p (c i) j -> p c j i", i=LINE),
                w2_raw[b][:, :, lo:hi].rearrange("p j (c i) -> p c j i", i=LINE),
            )

        def quantize_w2(b, lo, hi):
            quantize(w2_codes[b][:, lo:hi], w2_scales[b][:, lo:hi], w2_grouped[b][:, lo:hi, :].rearrange("p n j -> p (n j)"))

        def first_product(pre, b, t, c):
            w_cols = slice(t * P, (t + 1) * P)
            x_cols = slice(c * CHUNK, (c + 1) * CHUNK)
            for g in range(K_PASSES):
                nc.tensor.matmul_mx(
                    out=pre[:, t, :],
                    lhsT=w1_codes[b][g][:, w_cols].bitcast(FP8X4),
                    lhsT_scale=w1_scales[b][g][:, w_cols],
                    rhs=x_codes[g][:, x_cols].bitcast(FP8X4),
                    rhs_scale=x_scales[g][:, x_cols],
                    start=(g == 0),
                    stop=(g == K_PASSES - 1),
                )

        def gelu(pre, b, c):
            nc.scalar.activation(out=h_grouped[b][:, c * CHUNK : (c + 1) * CHUNK, :], in_=pre[:].rearrange("p t n -> p n t"), func=GELU)

        def quantize_h(b, lo, hi):
            quantize(h_codes[b][:, lo:hi], h_scales[b][:, lo:hi], h_grouped[b][:, lo:hi, :].rearrange("p n t -> p (n t)"))

        def second_pass(acc, b, m, v_cols):
            cols = slice(m * P, (m + 1) * P)
            nc.tensor.matmul_mx(
                out=acc,
                lhsT=w2_codes[b][:, cols].bitcast(FP8X4),
                lhsT_scale=w2_scales[b][:, cols],
                rhs=h_codes[b][:, v_cols].bitcast(FP8X4),
                rhs_scale=h_scales[b][:, v_cols],
                start=(b == 0),
                stop=(b == H_PASSES - 1),
            )

        warm_bank = psum.tile([P, V], F32, name="warm_bank", tag="acc0")

        def warm_up(codes, scales):
            for i in range(3):
                nc.tensor.matmul_mx(
                    out=warm_bank[:],
                    lhsT=codes[:, 0:P].bitcast(FP8X4),
                    lhsT_scale=scales[:, 0:P],
                    rhs=x_codes[0][:].bitcast(FP8X4),
                    rhs_scale=x_scales[0][:],
                    start=True,
                    stop=True,
                )

        half = V // 2
        nc.sync.dma_start(offsets[:], offs)
        for l in range(LEVELS):
            load_table(l)
        for b in range(H_PASSES):
            for g in range(K_PASSES):
                load_w1(b, g)
        load_w2(0, 0, N)
        load_w2(1, 0, half)
        load_w2(1, half, N)

        nc.vector.memset(warm_in[:], 0.0)
        nc.scalar.activation(out=warm_out[:], in_=warm_in[:], func=GELU)

        for l in range(PACK):
            gather(l, 0, V)
        group_x("scalar", 0, 0, V)
        gather(4, 0, V)
        gather(5, 0, V)
        quantize_x(0, 0, V)
        gather(6, 0, V)
        gather(7, half, V)
        gather(7, 0, half)
        group_x("scalar", 1, half, 384)
        group_x("vector", 1, 384, V)
        group_x("scalar", 1, 0, 192)
        group_x("vector", 1, 192, half)
        quantize_x(1, half, V)
        quantize_x(1, 0, half)

        group_w1("scalar", 0, 0, 0, 32)
        group_w1("vector", 0, 0, 32, P)
        quantize_w1(0, 0, 0, PACK)
        warm_up(w1_codes[0][0], w1_scales[0][0])
        group_w1("scalar", 0, 1, 0, 48)
        group_w1("vector", 0, 1, 48, P)
        quantize_w1(0, 1, 0, PACK)
        pres = [psum.tile([P, PACK, CHUNK], F32, name=f"pre0{c}", tag=f"pre{c}") for c in range(CHUNKS)]
        for c in range(CHUNKS):
            for t in range(PACK):
                first_product(pres[c], 0, t, c)
        group_w1("scalar", 1, 0, 0, 48)
        group_w1("vector", 1, 0, 48, P)
        quantize_w1(1, 0, 0, PACK)
        warm_up(w1_codes[1][0], w1_scales[1][0])
        gelu(pres[0], 0, 0)
        gelu(pres[1], 0, 1)
        group_w1("scalar", 1, 1, 0, 32)
        group_w1("vector", 1, 1, 32, P)
        gelu(pres[2], 0, 2)
        gelu(pres[3], 0, 3)
        quantize_w1(1, 1, 0, PACK // 2)
        quantize_w1(1, 1, PACK // 2, PACK)
        pres = [psum.tile([P, PACK, CHUNK], F32, name=f"pre1{c}", tag=f"pre{c}") for c in range(CHUNKS)]
        for c in range(CHUNKS):
            for t in range(PACK):
                first_product(pres[c], 1, t, c)
        group_w2("vector", 0, 0, N)
        quantize_h(0, 0, V)
        quantize_w2(0, 0, N)
        group_w2("vector", 1, 0, half)
        gelu(pres[0], 1, 0)
        gelu(pres[1], 1, 1)
        quantize_h(1, 0, half)
        quantize_w2(1, 0, half)
        gelu(pres[2], 1, 2)
        gelu(pres[3], 1, 3)
        quantize_h(1, half, V)
        group_w2("vector", 1, half + 192, N)
        group_w2("scalar", 1, half, half + 192)
        quantize_w2(1, half, N)
        accs = [psum.tile([P, V], F32, name=f"acc{m}") for m in range(OUT_BLOCKS)]
        for b in range(H_PASSES):
            for m in range(OUT_BLOCKS):
                second_pass(accs[m][:], b, m, slice(0, V))
        for m in range(OUT_BLOCKS):
            copy("scalar" if m % 2 == 0 else "vector", results[m][:], accs[m][:])
            nc.sync.dma_start(out=out[m * P : (m + 1) * P, :], in_=results[m][:])
